import numpy as np
import ml_dtypes


def mxq(x, axis, fmt="e4m3"):
    dtype, down = {"e4m3": (ml_dtypes.float8_e4m3fn, 7), "e5m2": (ml_dtypes.float8_e5m2, 14)}[fmt]
    v = np.moveaxis(np.asarray(x, np.float32).astype(ml_dtypes.bfloat16).astype(np.float64), axis, -1)
    blocks = v.reshape(v.shape[:-1] + (-1, 32))
    amax = np.abs(blocks).max(-1, keepdims=True)
    byte = np.maximum(np.where(amax > 0, np.frexp(amax)[1] - 1 + 127, 0) - down, 1)
    scale = np.exp2(byte - 127.0)
    codes = (blocks / scale).astype(np.float32).astype(dtype).astype(np.float64)
    return np.moveaxis((codes * scale).reshape(v.shape), -1, axis)


WIDE = False


def mx_kscale(k):
    if not WIDE:
        return np.ones(k)
    levels = np.array([10, -10, 5, -5, 0])
    if k % 512:
        return np.exp2(np.random.permutation(np.resize(levels, k // 32))).repeat(32)
    a = np.empty((k // 512, 16))
    for p in range(k // 512):
        a[p, :8] = np.random.permutation(np.resize(levels, 8))
        for g in range(8):
            far = levels[np.abs(levels - a[p, g]) >= 10]
            a[p, g + 8] = far[np.random.randint(len(far))]
    return np.exp2(a.ravel()).repeat(32)


def f64(x):
    return np.asarray(x).astype(np.float64)


def striped8(idx):
    return np.asarray(idx).reshape(8, -1, 16).transpose(0, 2, 1).reshape(128, -1).astype(np.uint16)


def unstriped8(offs):
    return offs.reshape(8, 16, -1).transpose(0, 2, 1).reshape(8, -1).astype(np.int64)


def pick8(x, idx, run):
    r = np.arange(len(x))
    return x[r[:, None], idx[r % (8 * run) // run]]


E2M1 = np.array([0.0, 0.5, 1.0, 1.5, 2.0, 3.0, 4.0, 6.0, -0.0, -0.5, -1.0, -1.5, -2.0, -3.0, -4.0, -6.0])


def pack_weight(w, fmt):
    k, n = w.shape
    w = f64(np.asarray(w, np.float32).astype(ml_dtypes.bfloat16)).reshape(k // 32, 32, n)
    amax = np.abs(w).max(1)
    if fmt == "e4m3":
        byte = np.frexp(amax)[1] - 1 + 127 - 7
    else:
        mant, ex = np.frexp(amax / 6.0)
        byte = np.where(mant > 0.5, ex, ex - 1) + 127
    byte = np.clip(np.where(amax > 0, byte, 1), 1, 254)
    scaled = (w * np.exp2(127.0 - byte)[:, None, :]).reshape(k, n).astype(np.float32)
    by_word = np.ascontiguousarray(scaled.reshape(k // 512, 128, 4, n).transpose(0, 1, 3, 2))
    if fmt == "e4m3":
        words = by_word.astype(ml_dtypes.float8_e4m3fn).view(np.uint8)
    else:
        c = by_word.astype(ml_dtypes.float4_e2m1fn).view(np.uint8) & 0xF
        words = (c[..., 0::2] | (c[..., 1::2] << 4)).reshape(k // 512, 128, 2 * n)
    return np.ascontiguousarray(words), np.ascontiguousarray(byte.astype(np.uint8).reshape(k // 512, 16, n))


def unpack_weight(words, scales, fmt):
    g, _, n = scales.shape
    words = np.ascontiguousarray(words).reshape(g, 128, n, -1)
    if fmt == "e4m3":
        vals = words.view(ml_dtypes.float8_e4m3fn).astype(np.float64)
    else:
        nib = np.empty((g, 128, n, 4), np.uint8)
        nib[..., 0::2] = words & 0xF
        nib[..., 1::2] = words >> 4
        vals = E2M1[nib]
    vals = vals * np.repeat(np.exp2(scales.astype(np.float64) - 127.0), 8, axis=1)[..., None]
    return vals.transpose(0, 1, 3, 2).reshape(g * 512, n)


D, T, I, Q, E = 512, 1024, 512, 512, 256


def setup_inputs():
    n = np.random.standard_normal
    idx = np.stack([np.random.permutation(T)[:I] for _ in range(8)])
    idx2 = np.stack([np.random.permutation(T)[:I] for _ in range(8)])
    idx3 = np.stack([np.random.permutation(T)[:I] for _ in range(8)])
    idx4 = np.stack([np.random.permutation(T)[:I] for _ in range(8)])
    fd = mx_kscale(D)
    fq = mx_kscale(Q)
    keysp = pack_weight(n((D, T)) / fd[:, None], "e2m1")
    mixp = pack_weight(n((Q, E)) * 1.0 / np.sqrt(Q) / fq[:, None], "e4m3")
    return {
        "query": (n((D, Q)) * 1.0 / np.sqrt(D) * fd[:, None]).astype(np.float32),
        "keys_words": keysp[0],
        "keys_scales": keysp[1],
        "lam": (np.random.uniform(0.3, 0.8, (Q, 1))).astype(np.float32),
        "rowf": (np.random.uniform(0.5, 2.0, (Q, 1)) * fq[:, None]).astype(np.float32),
        "mix_words": mixp[0],
        "mix_scales": mixp[1],
        "offs": striped8(idx),
        "offs2": striped8(idx2),
        "offs3": striped8(idx3),
        "offs4": striped8(idx4),
    }


def reference(query, keys_words, keys_scales, lam, rowf, mix_words, mix_scales, offs, offs2, offs3, offs4):
    idx = unstriped8(offs)
    idx2 = unstriped8(offs2)
    idx3 = unstriped8(offs3)
    idx4 = unstriped8(offs4)
    keysu = unpack_weight(keys_words, keys_scales, "e2m1")
    mixu = unpack_weight(mix_words, mix_scales, "e4m3")
    queryq = mxq(f64(query), 0, "e4m3")
    a = queryq.T @ keysu
    r = pick8(a, idx2, 64) - pick8(a, idx, 64)
    f1 = np.zeros((Q, T))
    f1[np.arange(Q)[:, None], idx[np.arange(Q) % 512 // 64]] = r
    c1 = a + f1 * f64(lam)
    v = pick8(c1, idx3, 64) - pick8(c1, idx4, 64)
    f2 = np.zeros((Q, T))
    f2[np.arange(Q)[:, None], idx4[np.arange(Q) % 512 // 64]] = v
    c2 = c1 + f2 * f64(lam)
    g = pick8(c2, idx2, 64)
    gw = g * f64(rowf)
    gwq = mxq(gw, 0, "e4m3")
    y = mixu.T @ gwq
    return y

@@ -1,0 +1,209 @@
+from contextlib import ExitStack
+
+import concourse.mybir as mybir
+
+D, T, I, Q, E = 512, 1024, 512, 512, 256
+FLOPS = 2 * D * Q * T + 2 * Q * E * I
+
+F32 = mybir.dt.float32
+BF16 = mybir.dt.bfloat16
+I32 = mybir.dt.int32
+U32 = mybir.dt.uint32
+U16 = mybir.dt.uint16
+U8 = mybir.dt.uint8
+FP8X4 = mybir.dt.float8_e4m3fn_x4
+FP4X4 = mybir.dt.float4_e2m1fn_x4
+MULT = mybir.AluOpType.mult
+ADD = mybir.AluOpType.add
+COPY = mybir.ActivationFunctionType.Copy
+
+P = 128
+PACK = 4
+BANK = 512
+HALF = I // 2
+LIST_COLS = I // 16
+HALF_COLS = LIST_COLS // 2
+
+
+def tile_attend_settledtwice_one_mixed_kernel(
+    tc, query, keys_words, keys_scales, lam, rowf, mix_words, mix_scales, offs, offs2, offs3, offs4, out
+):
+    nc = tc.nc
+    with ExitStack() as ctx:
+        keep = ctx.enter_context(tc.tile_pool(name="keep", bufs=1))
+        psum = ctx.enter_context(tc.psum_pool(name="psum", bufs=1))
+
+        def load_list(source, name):
+            offsets = keep.tile([P, LIST_COLS], U16, name=name)
+            nc.sync.dma_start(offsets[:], source)
+            return offsets
+
+        def load_scale_rows(queue, plane, source):
+            for r in range(4):
+                queue.dma_start(out=plane[r:P:32, :].bitcast(I32), in_=source[0, r:16:4, :].bitcast(I32))
+
+        key_scale = keep.tile([P, T], U8, align_bytes=64)
+        nc.vector.memset(key_scale[:].bitcast(I32), 0)
+        q_rows = query.rearrange("(p t) q -> p t q", t=PACK)
+        q_raw = [keep.tile([P, PACK, Q // 2], F32, name="q_raw%d" % h) for h in range(2)]
+        for h in range(2):
+            nc.sync.dma_start(out=q_raw[h][:], in_=q_rows[:, :, h * (Q // 2) : (h + 1) * (Q // 2)])
+        key_word = keep.tile([P, 2 * T], U8, align_bytes=64)
+        nc.sync.dma_start(out=key_word[:], in_=keys_words[0])
+        load_scale_rows(nc.scalar, key_scale, keys_scales)
+        list1 = load_list(offs, "list1")
+        list2 = load_list(offs2, "list2")
+        lam_sb = keep.tile([P, PACK], F32)
+        nc.sync.dma_start(out=lam_sb[:], in_=lam.rearrange("(p j) o -> p (j o)", j=PACK))
+        list3 = load_list(offs3, "list3")
+        list4 = load_list(offs4, "list4")
+        rowf_sb = keep.tile([P, PACK], F32)
+        nc.sync.dma_start(out=rowf_sb[:], in_=rowf.rearrange("(p j) o -> p (j o)", j=PACK))
+        mix_word = keep.tile([P, E], U32, align_bytes=64)
+        nc.sync.dma_start(out=mix_word[:].bitcast(I32), in_=mix_words[0].rearrange("p n t -> p (n t)").bitcast(I32))
+        mix_scale = keep.tile([P, E], U8, align_bytes=64)
+        nc.vector.memset(mix_scale[:].bitcast(I32), 0)
+        load_scale_rows(nc.sync, mix_scale, mix_scales)
+
+        placed1 = [keep.tile([P, T], F32, name="placed1_%d" % b) for b in range(3)]
+        for tile in placed1:
+            nc.vector.memset(tile[:], 0.0)
+
+        q_bf = keep.tile([P, PACK, P, PACK], BF16, name="q_bf", align_bytes=64)
+        for h in range(2):
+            nc.vector.tensor_copy(
+                out=q_bf[:, :, h * (P // 2) : (h + 1) * (P // 2), :].rearrange("p j m t -> p m t j"),
+                in_=q_raw[h][:].rearrange("p t (m j) -> p m t j", j=PACK),
+            )
+        q_code = keep.tile([P, Q], U32, align_bytes=64)
+        q_scale = keep.tile([P, Q], U8, align_bytes=64)
+        q_flat = q_bf[:].rearrange("p j m t -> p (j m t)")
+        for lo, hi in ((0, P), (P, Q)):
+            nc.vector.quantize_mx(
+                out=q_code[:, lo:hi].bitcast(FP8X4), scales=q_scale[:, lo:hi], in_=q_flat[:, PACK * lo : PACK * hi]
+            )
+
+        a_bank = [[psum.tile([P, BANK], F32, name="bank%d" % (2 * j + h)) for h in range(2)] for j in range(PACK)]
+        for j in range(PACK):
+            for h in range(2):
+                nc.tensor.matmul_mx(
+                    out=a_bank[j][h][:],
+                    lhsT=q_code[:, j * P : (j + 1) * P].bitcast(FP8X4),
+                    lhsT_scale=q_scale[:, j * P : (j + 1) * P],
+                    rhs=key_word[:, 2 * BANK * h : 2 * BANK * (h + 1)].bitcast(FP4X4),
+                    rhs_scale=key_scale[:, BANK * h : BANK * (h + 1)],
+                    start=True,
+                    stop=True,
+                )
+
+        a_sb, c1, c2 = {}, {}, {}
+        towards, negated = {}, {}
+
+        def fetch_pair(step, j, window, towards_list, moved_list):
+            towards[step, j] = keep.tile([P, I], F32, name="towards%d_%d" % (step, j))
+            negated[step, j] = keep.tile([P, I], F32, name="negated%d_%d" % (step, j))
+            nc.scalar.activation(negated[step, j][:], window[:].indirect(moved_list[:]), COPY, scale=-1.0)
+            nc.scalar.activation(towards[step, j][:], window[:].indirect(towards_list[:]), COPY)
+
+        def place(step, j, window, moved_list):
+            nc.vector.tensor_tensor(window[:].indirect(moved_list[:]), towards[step, j][:], negated[step, j][:], ADD)
+
+        def scores_out(j):
+            a_sb[j] = keep.tile([P, T], F32, name="wide%d" % j)
+            for h in range(2):
+                nc.scalar.copy(out=a_sb[j][:, BANK * h : BANK * (h + 1)], in_=a_bank[j][h][:])
+
+        def settle1(j, placed, tag):
+            c1[j] = keep.tile([P, T], F32, name=tag)
+            for h in range(2):
+                cols = slice(BANK * h, BANK * (h + 1))
+                nc.vector.scalar_tensor_tensor(c1[j][:, cols], placed[:, cols], lam_sb[:, j : j + 1], a_bank[j][h][:], MULT, ADD)
+
+        def settle2(j):
+            c2[j] = keep.tile([P, T], F32, name="c2_%d" % j)
+            nc.vector.scalar_tensor_tensor(c2[j][:], placed2[j % 3][:], lam_sb[:, j : j + 1], c1[j][:], MULT, ADD)
+
+        a_sb[0] = keep.tile([P, T], F32, name="wide0")
+        nc.vector.tensor_copy(out=a_sb[0][:, :BANK], in_=a_bank[0][0][:])
+        nc.scalar.copy(out=a_sb[0][:, BANK:], in_=a_bank[0][1][:])
+        first_towards = [keep.tile([P, HALF], F32, name="first_towards%d" % h) for h in range(2)]
+        first_negated = [keep.tile([P, HALF], F32, name="first_negated%d" % h) for h in range(2)]
+        for h in range(2):
+            cols = slice(HALF_COLS * h, HALF_COLS * (h + 1))
+            nc.scalar.activation(first_negated[h][:], a_sb[0][:].indirect(list1[:, cols]), COPY, scale=-1.0)
+            if h == 0:
+                nc.vector.tensor_copy(first_towards[h][:], a_sb[0][:].indirect(list2[:, cols]))
+            else:
+                nc.scalar.activation(first_towards[h][:], a_sb[0][:].indirect(list2[:, cols]), COPY)
+            nc.vector.tensor_tensor(placed1[0][:].indirect(list1[:, cols]), first_towards[h][:], first_negated[h][:], ADD)
+        settle1(0, placed1[0], "c1_0")
+
+        scores_out(1)
+        fetch_pair(1, 1, a_sb[1], list2, list1)
+        place(1, 1, placed1[1], list1)
+        scores_out(2)
+        fetch_pair(1, 2, a_sb[2], list2, list1)
+        place(1, 2, placed1[0], list1)
+        settle1(1, placed1[1], "wide2")
+        scores_out(3)
+        fetch_pair(1, 3, a_sb[3], list2, list1)
+        place(1, 3, placed1[2], list1)
+        settle1(2, placed1[0], "wide3")
+
+        placed2 = [
+            keep.tile([P, T], F32, name="q_bf", align_bytes=64),
+            keep.tile([P, T], F32, name="wide0"),
+            keep.tile([P, T], F32, name="wide1"),
+        ]
+        for tile in placed2:
+            nc.gpsimd.memset(tile[:], 0.0)
+        fetch_pair(2, 0, c1[0], list3, list4)
+        place(2, 0, placed2[0], list4)
+        settle1(3, placed1[2], "c1_3")
+        for j in range(1, PACK):
+            fetch_pair(2, j, c1[j], list3, list4)
+            place(2, j, placed2[j % 3], list4)
+            settle2(j - 1)
+        settle2(PACK - 1)
+
+        last = PACK - 1
+        rowf_wide = keep.tile([P, HALF], F32)
+        nc.scalar.copy(out=rowf_wide[:], in_=rowf_sb[:, last : last + 1].to_broadcast([P, HALF]))
+        gw_low = keep.tile([P, PACK, HALF], F32)
+        gw_bf = [keep.tile([P, HALF, PACK], BF16, name="gw_bf%d" % h, align_bytes=64) for h in range(2)]
+        for j in range(last):
+            g = keep.tile([P, I], F32, name="g%d" % j)
+            nc.scalar.activation(g[:], c2[j][:].indirect(list2[:]), COPY)
+            nc.scalar.activation(gw_low[:, j, :], g[:, :HALF], COPY, scale=rowf_sb[:, j : j + 1])
+            nc.scalar.activation(gw_bf[1][:, :, j], g[:, HALF:], COPY, scale=rowf_sb[:, j : j + 1])
+        nc.vector.tensor_tensor(gw_low[:, last, :], c2[last][:].indirect(list2[:, :HALF_COLS]), rowf_wide[:], MULT)
+        g_last = keep.tile([P, HALF], F32)
+        nc.scalar.activation(g_last[:], c2[last][:].indirect(list2[:, HALF_COLS:]), COPY)
+        nc.scalar.activation(gw_bf[1][:, :, last], g_last[:], COPY, scale=rowf_sb[:, last : last + 1])
+        nc.vector.tensor_copy(
+            out=gw_bf[0][:].rearrange("p (c i) t -> p c t i", i=4),
+            in_=gw_low[:].rearrange("p t (c i) -> p c t i", i=4),
+        )
+        for h in range(2):
+            gw_code = keep.tile([P, HALF], U32, name="gw_code%d" % h, align_bytes=64)
+            gw_scale = keep.tile([P, HALF], U8, name="gw_scale%d" % h, align_bytes=64)
+            nc.vector.quantize_mx(
+                out=gw_code[:].bitcast(FP8X4), scales=gw_scale[:], in_=gw_bf[h][:].rearrange("p i t -> p (i t)")
+            )
+            for e in range(E // P):
+                y_bank = psum.tile([P, HALF], F32, name="bank%d" % (2 * h + e))
+                nc.tensor.matmul_mx(
+                    out=y_bank[:],
+                    lhsT=mix_word[:, e * P : (e + 1) * P].bitcast(FP8X4),
+                    lhsT_scale=mix_scale[:, e * P : (e + 1) * P],
+                    rhs=gw_code[:].bitcast(FP8X4),
+                    rhs_scale=gw_scale[:],
+                    start=True,
+                    stop=True,
+                )
+                y = keep.tile([P, HALF], F32, name="y%d_%d" % (h, e))
+                if h == 1 and e == 1:
+                    nc.vector.tensor_copy(out=y[:], in_=y_bank[:])
+                else:
+                    nc.scalar.copy(out=y[:], in_=y_bank[:])
+                nc.sync.dma_start(out=out[e * P : (e + 1) * P, h * HALF : (h + 1) * HALF], in_=y[:])

@@ -100,13 +100,22 @@ def tile_attend_settledtwice_one_mixed_kernel(
         towards, negated = {}, {}
 
         def fetch_pair(step, j, window, towards_list, moved_list):
-            towards[step, j] = keep.tile([P, I], F32, name="towards%d_%d" % (step, j))
-            negated[step, j] = keep.tile([P, I], F32, name="negated%d_%d" % (step, j))
-            nc.scalar.activation(negated[step, j][:], window[:].indirect(moved_list[:]), COPY, scale=-1.0)
-            nc.scalar.activation(towards[step, j][:], window[:].indirect(towards_list[:]), COPY)
+            pair = keep.tile([P, 2, I], F32, name="pair%d_%d" % (step, j))
+            negated[step, j], towards[step, j] = pair[:, 0, :], pair[:, 1, :]
+            nc.scalar.activation(negated[step, j], window[:].indirect(moved_list[:]), COPY, scale=-1.0)
+            nc.scalar.activation(towards[step, j], window[:].indirect(towards_list[:]), COPY)
 
         def place(step, j, window, moved_list):
-            nc.vector.tensor_tensor(window[:].indirect(moved_list[:]), towards[step, j][:], negated[step, j][:], ADD)
+            nc.vector.tensor_tensor(window[:].indirect(moved_list[:]), towards[step, j], negated[step, j], ADD)
+
+        def place_difference(step, j, window, moved_list, scaled):
+            diff = keep.tile([P, I], F32, name="diff%d_%d" % (step, j))
+            nc.gpsimd.tensor_tensor(diff[:], towards[step, j], negated[step, j], ADD)
+            if scaled:
+                moved_by = keep.tile([P, I], F32, name="moved_by%d_%d" % (step, j))
+                nc.gpsimd.tensor_scalar(moved_by[:], diff[:], lam_sb[:, j : j + 1], 0.0, MULT, ADD)
+                diff = moved_by
+            nc.vector.tensor_copy(window[:].indirect(moved_list[:]), diff[:])
 
         def scores_out(j):
             a_sb[j] = keep.tile([P, T], F32, name="wide%d" % j)
@@ -120,8 +129,11 @@ def tile_attend_settledtwice_one_mixed_kernel(
                 nc.vector.scalar_tensor_tensor(c1[j][:, cols], placed[:, cols], lam_sb[:, j : j + 1], a_bank[j][h][:], MULT, ADD)
 
         def settle2(j):
-            c2[j] = keep.tile([P, T], F32, name="c2_%d" % j)
-            nc.vector.scalar_tensor_tensor(c2[j][:], placed2[j % 3][:], lam_sb[:, j : j + 1], c1[j][:], MULT, ADD)
+            c2[j] = keep.tile([P, T], F32, name=("pair2_2", "pair2_3", "c2_2", "c2_3")[j])
+            if j == PACK - 1:
+                nc.vector.scalar_tensor_tensor(c2[j][:], placed2[j % 3][:], lam_sb[:, j : j + 1], c1[j][:], MULT, ADD)
+            else:
+                nc.gpsimd.tensor_tensor(c2[j][:], placed2[j % 3][:], c1[j][:], ADD)
 
         a_sb[0] = keep.tile([P, T], F32, name="wide0")
         nc.vector.tensor_copy(out=a_sb[0][:, :BANK], in_=a_bank[0][0][:])
@@ -141,14 +153,14 @@ def tile_attend_settledtwice_one_mixed_kernel(
         scores_out(1)
         fetch_pair(1, 1, a_sb[1], list2, list1)
         place(1, 1, placed1[1], list1)
+        settle1(1, placed1[1], "c1_1")
         scores_out(2)
         fetch_pair(1, 2, a_sb[2], list2, list1)
-        place(1, 2, placed1[0], list1)
-        settle1(1, placed1[1], "wide2")
+        place_difference(1, 2, placed1[0], list1, False)
         scores_out(3)
         fetch_pair(1, 3, a_sb[3], list2, list1)
-        place(1, 3, placed1[2], list1)
-        settle1(2, placed1[0], "wide3")
+        place_difference(1, 3, placed1[2], list1, False)
+        settle1(2, placed1[0], "pair1_3")
 
         placed2 = [
             keep.tile([P, T], F32, name="q_bf", align_bytes=64),
@@ -158,13 +170,16 @@ def tile_attend_settledtwice_one_mixed_kernel(
         for tile in placed2:
             nc.gpsimd.memset(tile[:], 0.0)
         fetch_pair(2, 0, c1[0], list3, list4)
-        place(2, 0, placed2[0], list4)
-        settle1(3, placed1[2], "c1_3")
-        for j in range(1, PACK):
+        place_difference(2, 0, placed2[0], list4, True)
+        settle1(3, placed1[2], "pair2_0")
+        for j in range(1, PACK - 1):
             fetch_pair(2, j, c1[j], list3, list4)
-            place(2, j, placed2[j % 3], list4)
-            settle2(j - 1)
-        settle2(PACK - 1)
+            place_difference(2, j, placed2[j], list4, True)
+        settle2(0)
+        fetch_pair(2, PACK - 1, c1[PACK - 1], list3, list4)
+        place_difference(2, PACK - 1, placed2[0], list4, False)
+        for j in range(1, PACK):
+            settle2(j)
 
         last = PACK - 1
         rowf_wide = keep.tile([P, HALF], F32)

@@ -65,20 +65,25 @@ def tile_attend_settledtwice_one_mixed_kernel(
         nc.vector.memset(mix_scale[:].bitcast(I32), 0)
         load_scale_rows(nc.sync, mix_scale, mix_scales)
 
-        placed1 = [keep.tile([P, T], F32, name="placed1_%d" % b) for b in range(3)]
+        placed1 = [keep.tile([P, T], F32, name="placed1_%d" % b) for b in range(2)]
         for tile in placed1:
             nc.vector.memset(tile[:], 0.0)
 
         q_bf = keep.tile([P, PACK, P, PACK], BF16, name="q_bf", align_bytes=64)
-        for h in range(2):
+
+        def deal_query(h, tiles):
             nc.vector.tensor_copy(
-                out=q_bf[:, :, h * (P // 2) : (h + 1) * (P // 2), :].rearrange("p j m t -> p m t j"),
-                in_=q_raw[h][:].rearrange("p t (m j) -> p m t j", j=PACK),
+                out=q_bf[:, tiles, h * (P // 2) : (h + 1) * (P // 2), :].rearrange("p j m t -> p m t j"),
+                in_=q_raw[h][:].rearrange("p t (m j) -> p m t j", j=PACK)[:, :, :, tiles],
             )
+
         q_code = keep.tile([P, Q], U32, align_bytes=64)
         q_scale = keep.tile([P, Q], U8, align_bytes=64)
         q_flat = q_bf[:].rearrange("p j m t -> p (j m t)")
-        for lo, hi in ((0, P), (P, Q)):
+        for tiles in (slice(0, 1), slice(1, PACK)):
+            lo, hi = P * tiles.start, P * tiles.stop
+            for h in range(2):
+                deal_query(h, tiles)
             nc.vector.quantize_mx(
                 out=q_code[:, lo:hi].bitcast(FP8X4), scales=q_scale[:, lo:hi], in_=q_flat[:, PACK * lo : PACK * hi]
             )
@@ -109,7 +114,7 @@ def tile_attend_settledtwice_one_mixed_kernel(
             nc.vector.tensor_tensor(window[:].indirect(moved_list[:]), towards[step, j], negated[step, j], ADD)
 
         def place_difference(step, j, window, moved_list, scaled):
-            diff = keep.tile([P, I], F32, name="diff%d_%d" % (step, j))
+            diff = keep.tile([P, I], F32, name="diff%d" % step)
             nc.gpsimd.tensor_tensor(diff[:], towards[step, j], negated[step, j], ADD)
             if scaled:
                 moved_by = keep.tile([P, I], F32, name="moved_by%d_%d" % (step, j))
@@ -117,10 +122,13 @@ def tile_attend_settledtwice_one_mixed_kernel(
                 diff = moved_by
             nc.vector.tensor_copy(window[:].indirect(moved_list[:]), diff[:])
 
-        def scores_out(j):
+        def scores_out(j, shared):
             a_sb[j] = keep.tile([P, T], F32, name="wide%d" % j)
-            for h in range(2):
-                nc.scalar.copy(out=a_sb[j][:, BANK * h : BANK * (h + 1)], in_=a_bank[j][h][:])
+            if shared:
+                nc.vector.tensor_copy(out=a_sb[j][:, :BANK], in_=a_bank[j][0][:])
+            else:
+                nc.scalar.copy(out=a_sb[j][:, :BANK], in_=a_bank[j][0][:])
+            nc.scalar.copy(out=a_sb[j][:, BANK:], in_=a_bank[j][1][:])
 
         def settle1(j, placed, tag):
             c1[j] = keep.tile([P, T], F32, name=tag)
@@ -129,15 +137,13 @@ def tile_attend_settledtwice_one_mixed_kernel(
                 nc.vector.scalar_tensor_tensor(c1[j][:, cols], placed[:, cols], lam_sb[:, j : j + 1], a_bank[j][h][:], MULT, ADD)
 
         def settle2(j):
-            c2[j] = keep.tile([P, T], F32, name=("pair2_2", "pair2_3", "c2_2", "c2_3")[j])
+            c2[j] = keep.tile([P, T], F32, name="c1_%d" % (j - 1) if j else "pair2_3")
             if j == PACK - 1:
                 nc.vector.scalar_tensor_tensor(c2[j][:], placed2[j % 3][:], lam_sb[:, j : j + 1], c1[j][:], MULT, ADD)
             else:
                 nc.gpsimd.tensor_tensor(c2[j][:], placed2[j % 3][:], c1[j][:], ADD)
 
-        a_sb[0] = keep.tile([P, T], F32, name="wide0")
-        nc.vector.tensor_copy(out=a_sb[0][:, :BANK], in_=a_bank[0][0][:])
-        nc.scalar.copy(out=a_sb[0][:, BANK:], in_=a_bank[0][1][:])
+        scores_out(0, True)
         first_towards = [keep.tile([P, HALF], F32, name="first_towards%d" % h) for h in range(2)]
         first_negated = [keep.tile([P, HALF], F32, name="first_negated%d" % h) for h in range(2)]
         for h in range(2):
@@ -147,20 +153,22 @@ def tile_attend_settledtwice_one_mixed_kernel(
                 nc.vector.tensor_copy(first_towards[h][:], a_sb[0][:].indirect(list2[:, cols]))
             else:
                 nc.scalar.activation(first_towards[h][:], a_sb[0][:].indirect(list2[:, cols]), COPY)
+            if h == 1:
+                scores_out(1, True)
             nc.vector.tensor_tensor(placed1[0][:].indirect(list1[:, cols]), first_towards[h][:], first_negated[h][:], ADD)
         settle1(0, placed1[0], "c1_0")
 
-        scores_out(1)
         fetch_pair(1, 1, a_sb[1], list2, list1)
         place(1, 1, placed1[1], list1)
         settle1(1, placed1[1], "c1_1")
-        scores_out(2)
+        scores_out(2, False)
         fetch_pair(1, 2, a_sb[2], list2, list1)
-        place_difference(1, 2, placed1[0], list1, False)
-        scores_out(3)
+        place(1, 2, placed1[0], list1)
+        settle1(2, placed1[0], "c1_2")
+        scores_out(3, False)
         fetch_pair(1, 3, a_sb[3], list2, list1)
-        place_difference(1, 3, placed1[2], list1, False)
-        settle1(2, placed1[0], "pair1_3")
+        place_difference(1, 3, placed1[1], list1, False)
+        settle1(3, placed1[1], "c1_3")
 
         placed2 = [
             keep.tile([P, T], F32, name="q_bf", align_bytes=64),
@@ -169,15 +177,14 @@ def tile_attend_settledtwice_one_mixed_kernel(
         ]
         for tile in placed2:
             nc.gpsimd.memset(tile[:], 0.0)
-        fetch_pair(2, 0, c1[0], list3, list4)
-        place_difference(2, 0, placed2[0], list4, True)
-        settle1(3, placed1[2], "pair2_0")
-        for j in range(1, PACK - 1):
+        for j in range(PACK - 1):
             fetch_pair(2, j, c1[j], list3, list4)
             place_difference(2, j, placed2[j], list4, True)
-        settle2(0)
         fetch_pair(2, PACK - 1, c1[PACK - 1], list3, list4)
-        place_difference(2, PACK - 1, placed2[0], list4, False)
+        last_diff = keep.tile([P, I], F32, name="diff2")
+        nc.gpsimd.tensor_tensor(last_diff[:], towards[2, PACK - 1], negated[2, PACK - 1], ADD)
+        settle2(0)
+        nc.vector.tensor_copy(placed2[0][:].indirect(list4[:]), last_diff[:])
         for j in range(1, PACK):
             settle2(j)
 
@@ -189,7 +196,10 @@ def tile_attend_settledtwice_one_mixed_kernel(
         for j in range(last):
             g = keep.tile([P, I], F32, name="g%d" % j)
             nc.scalar.activation(g[:], c2[j][:].indirect(list2[:]), COPY)
-            nc.scalar.activation(gw_low[:, j, :], g[:, :HALF], COPY, scale=rowf_sb[:, j : j + 1])
+            if j < last - 1:
+                nc.scalar.activation(gw_low[:, j, :], g[:, :HALF], COPY, scale=rowf_sb[:, j : j + 1])
+            else:
+                nc.vector.tensor_scalar(gw_low[:, j, :], g[:, :HALF], rowf_sb[:, j : j + 1], None, MULT)
             nc.scalar.activation(gw_bf[1][:, :, j], g[:, HALF:], COPY, scale=rowf_sb[:, j : j + 1])
         nc.vector.tensor_tensor(gw_low[:, last, :], c2[last][:].indirect(list2[:, :HALF_COLS]), rowf_wide[:], MULT)
         g_last = keep.tile([P, HALF], F32)
@@ -221,4 +231,5 @@ def tile_attend_settledtwice_one_mixed_kernel(
                     nc.vector.tensor_copy(out=y[:], in_=y_bank[:])
                 else:
                     nc.scalar.copy(out=y[:], in_=y_bank[:])
-                nc.sync.dma_start(out=out[e * P : (e + 1) * P, h * HALF : (h + 1) * HALF], in_=y[:])
+                queue = nc.scalar if h == 1 and e == 0 else nc.sync
+                queue.dma_start(out=out[e * P : (e + 1) * P, h * HALF : (h + 1) * HALF], in_=y[:])

@@ -23,6 +23,8 @@ BANK = 512
 HALF = I // 2
 LIST_COLS = I // 16
 HALF_COLS = LIST_COLS // 2
+QUARTER = I // 4
+QUARTER_COLS = LIST_COLS // 4
 
 
 def tile_attend_settledtwice_one_mixed_kernel(
@@ -48,9 +50,9 @@ def tile_attend_settledtwice_one_mixed_kernel(
         q_raw = [keep.tile([P, PACK, Q // 2], F32, name="q_raw%d" % h) for h in range(2)]
         for h in range(2):
             nc.sync.dma_start(out=q_raw[h][:], in_=q_rows[:, :, h * (Q // 2) : (h + 1) * (Q // 2)])
+        load_scale_rows(nc.sync, key_scale, keys_scales)
         key_word = keep.tile([P, 2 * T], U8, align_bytes=64)
         nc.sync.dma_start(out=key_word[:], in_=keys_words[0])
-        load_scale_rows(nc.scalar, key_scale, keys_scales)
         list1 = load_list(offs, "list1")
         list2 = load_list(offs2, "list2")
         lam_sb = keep.tile([P, PACK], F32)
@@ -137,7 +139,7 @@ def tile_attend_settledtwice_one_mixed_kernel(
                 nc.vector.scalar_tensor_tensor(c1[j][:, cols], placed[:, cols], lam_sb[:, j : j + 1], a_bank[j][h][:], MULT, ADD)
 
         def settle2(j):
-            c2[j] = keep.tile([P, T], F32, name="c1_%d" % (j - 1) if j else "pair2_3")
+            c2[j] = keep.tile([P, T], F32, name=("pair2_3", "c1_0", "wide2", "c1_2")[j])
             if j == PACK - 1:
                 nc.vector.scalar_tensor_tensor(c2[j][:], placed2[j % 3][:], lam_sb[:, j : j + 1], c1[j][:], MULT, ADD)
             else:
@@ -154,16 +156,16 @@ def tile_attend_settledtwice_one_mixed_kernel(
             else:
                 nc.scalar.activation(first_towards[h][:], a_sb[0][:].indirect(list2[:, cols]), COPY)
             if h == 1:
-                scores_out(1, True)
+                scores_out(1, False)
             nc.vector.tensor_tensor(placed1[0][:].indirect(list1[:, cols]), first_towards[h][:], first_negated[h][:], ADD)
         settle1(0, placed1[0], "c1_0")
 
         fetch_pair(1, 1, a_sb[1], list2, list1)
         place(1, 1, placed1[1], list1)
-        settle1(1, placed1[1], "c1_1")
         scores_out(2, False)
         fetch_pair(1, 2, a_sb[2], list2, list1)
         place(1, 2, placed1[0], list1)
+        settle1(1, placed1[1], "wide2")
         settle1(2, placed1[0], "c1_2")
         scores_out(3, False)
         fetch_pair(1, 3, a_sb[3], list2, list1)
@@ -189,9 +191,9 @@ def tile_attend_settledtwice_one_mixed_kernel(
             settle2(j)
 
         last = PACK - 1
-        rowf_wide = keep.tile([P, HALF], F32)
-        nc.scalar.copy(out=rowf_wide[:], in_=rowf_sb[:, last : last + 1].to_broadcast([P, HALF]))
-        gw_low = keep.tile([P, PACK, HALF], F32)
+        rowf_wide = keep.tile([P, QUARTER], F32)
+        nc.scalar.copy(out=rowf_wide[:], in_=rowf_sb[:, last : last + 1].to_broadcast([P, QUARTER]))
+        gw_low = keep.tile([P, PACK, HALF], F32, name="gw_low", align_bytes=64)
         gw_bf = [keep.tile([P, HALF, PACK], BF16, name="gw_bf%d" % h, align_bytes=64) for h in range(2)]
         for j in range(last):
             g = keep.tile([P, I], F32, name="g%d" % j)
@@ -201,20 +203,32 @@ def tile_attend_settledtwice_one_mixed_kernel(
             else:
                 nc.vector.tensor_scalar(gw_low[:, j, :], g[:, :HALF], rowf_sb[:, j : j + 1], None, MULT)
             nc.scalar.activation(gw_bf[1][:, :, j], g[:, HALF:], COPY, scale=rowf_sb[:, j : j + 1])
-        nc.vector.tensor_tensor(gw_low[:, last, :], c2[last][:].indirect(list2[:, :HALF_COLS]), rowf_wide[:], MULT)
+        for u in range(2):
+            nc.vector.tensor_tensor(
+                gw_low[:, last, QUARTER * u : QUARTER * (u + 1)],
+                c2[last][:].indirect(list2[:, QUARTER_COLS * u : QUARTER_COLS * (u + 1)]),
+                rowf_wide[:],
+                MULT,
+            )
         g_last = keep.tile([P, HALF], F32)
         nc.scalar.activation(g_last[:], c2[last][:].indirect(list2[:, HALF_COLS:]), COPY)
         nc.scalar.activation(gw_bf[1][:, :, last], g_last[:], COPY, scale=rowf_sb[:, last : last + 1])
-        nc.vector.tensor_copy(
-            out=gw_bf[0][:].rearrange("p (c i) t -> p c t i", i=4),
-            in_=gw_low[:].rearrange("p t (c i) -> p c t i", i=4),
-        )
-        for h in range(2):
-            gw_code = keep.tile([P, HALF], U32, name="gw_code%d" % h, align_bytes=64)
-            gw_scale = keep.tile([P, HALF], U8, name="gw_scale%d" % h, align_bytes=64)
-            nc.vector.quantize_mx(
-                out=gw_code[:].bitcast(FP8X4), scales=gw_scale[:], in_=gw_bf[h][:].rearrange("p i t -> p (i t)")
+        for u in range(2):
+            slots = slice(QUARTER * u, QUARTER * (u + 1))
+            nc.vector.tensor_copy(
+                out=gw_bf[0][:, slots, :].rearrange("p (c i) t -> p c t i", i=4),
+                in_=gw_low[:, :, slots].rearrange("p t (c i) -> p c t i", i=4),
             )
+        for h in range(2):
+            gw_code = keep.tile([P, HALF], U32, name="gw_low" if h else "gw_code0", align_bytes=64)
+            gw_scale = keep.tile([P, HALF], U8, name="gw_scale%d" % h, align_bytes=64)
+            width = HALF if h else QUARTER
+            for lo in range(0, HALF, width):
+                nc.vector.quantize_mx(
+                    out=gw_code[:, lo : lo + width].bitcast(FP8X4),
+                    scales=gw_scale[:, lo : lo + width],
+                    in_=gw_bf[h][:, lo : lo + width, :].rearrange("p i t -> p (i t)"),
+                )
             for e in range(E // P):
                 y_bank = psum.tile([P, HALF], F32, name="bank%d" % (2 * h + e))
                 nc.tensor.matmul_mx(

from contextlib import ExitStack

import concourse.mybir as mybir

D, T, I, Q, E = 512, 1024, 512, 512, 256
FLOPS = 2 * D * Q * T + 2 * Q * E * I

F32 = mybir.dt.float32
BF16 = mybir.dt.bfloat16
I32 = mybir.dt.int32
U32 = mybir.dt.uint32
U16 = mybir.dt.uint16
U8 = mybir.dt.uint8
FP8X4 = mybir.dt.float8_e4m3fn_x4
FP4X4 = mybir.dt.float4_e2m1fn_x4
MULT = mybir.AluOpType.mult
ADD = mybir.AluOpType.add
COPY = mybir.ActivationFunctionType.Copy

P = 128
PACK = 4
BANK = 512
HALF = I // 2
LIST_COLS = I // 16
HALF_COLS = LIST_COLS // 2
QUARTER = I // 4
QUARTER_COLS = LIST_COLS // 4


def tile_attend_settledtwice_one_mixed_kernel(
    tc, query, keys_words, keys_scales, lam, rowf, mix_words, mix_scales, offs, offs2, offs3, offs4, out
):
    nc = tc.nc
    with ExitStack() as ctx:
        keep = ctx.enter_context(tc.tile_pool(name="keep", bufs=1))
        psum = ctx.enter_context(tc.psum_pool(name="psum", bufs=1))

        def load_list(source, name):
            offsets = keep.tile([P, LIST_COLS], U16, name=name)
            nc.sync.dma_start(offsets[:], source)
            return offsets

        def load_scale_rows(queue, plane, source):
            for r in range(4):
                queue.dma_start(out=plane[r:P:32, :].bitcast(I32), in_=source[0, r:16:4, :].bitcast(I32))

        key_scale = keep.tile([P, T], U8, align_bytes=64)
        nc.vector.memset(key_scale[:].bitcast(I32), 0)
        q_rows = query.rearrange("(p t) q -> p t q", t=PACK)
        q_raw = [keep.tile([P, PACK, Q // 2], F32, name="q_raw%d" % h) for h in range(2)]
        for h in range(2):
            nc.sync.dma_start(out=q_raw[h][:], in_=q_rows[:, :, h * (Q // 2) : (h + 1) * (Q // 2)])
        load_scale_rows(nc.sync, key_scale, keys_scales)
        key_word = keep.tile([P, 2 * T], U8, align_bytes=64)
        nc.sync.dma_start(out=key_word[:], in_=keys_words[0])
        list1 = load_list(offs, "list1")
        list2 = load_list(offs2, "list2")
        lam_sb = keep.tile([P, PACK], F32)
        nc.sync.dma_start(out=lam_sb[:], in_=lam.rearrange("(p j) o -> p (j o)", j=PACK))
        list3 = load_list(offs3, "list3")
        list4 = load_list(offs4, "list4")
        rowf_sb = keep.tile([P, PACK], F32)
        nc.sync.dma_start(out=rowf_sb[:], in_=rowf.rearrange("(p j) o -> p (j o)", j=PACK))
        mix_word = keep.tile([P, E], U32, align_bytes=64)
        nc.sync.dma_start(out=mix_word[:].bitcast(I32), in_=mix_words[0].rearrange("p n t -> p (n t)").bitcast(I32))
        mix_scale = keep.tile([P, E], U8, align_bytes=64)
        nc.vector.memset(mix_scale[:].bitcast(I32), 0)
        load_scale_rows(nc.sync, mix_scale, mix_scales)

        placed1 = [keep.tile([P, T], F32, name="placed1_%d" % b) for b in range(2)]
        for tile in placed1:
            nc.vector.memset(tile[:], 0.0)

        q_bf = keep.tile([P, PACK, P, PACK], BF16, name="q_bf", align_bytes=64)

        def deal_query(h, tiles):
            nc.vector.tensor_copy(
                out=q_bf[:, tiles, h * (P // 2) : (h + 1) * (P // 2), :].rearrange("p j m t -> p m t j"),
                in_=q_raw[h][:].rearrange("p t (m j) -> p m t j", j=PACK)[:, :, :, tiles],
            )

        q_code = keep.tile([P, Q], U32, align_bytes=64)
        q_scale = keep.tile([P, Q], U8, align_bytes=64)
        q_flat = q_bf[:].rearrange("p j m t -> p (j m t)")
        for tiles in (slice(0, 1), slice(1, PACK)):
            lo, hi = P * tiles.start, P * tiles.stop
            for h in range(2):
                deal_query(h, tiles)
            nc.vector.quantize_mx(
                out=q_code[:, lo:hi].bitcast(FP8X4), scales=q_scale[:, lo:hi], in_=q_flat[:, PACK * lo : PACK * hi]
            )

        a_bank = [[psum.tile([P, BANK], F32, name="bank%d" % (2 * j + h)) for h in range(2)] for j in range(PACK)]
        for j in range(PACK):
            for h in range(2):
                nc.tensor.matmul_mx(
                    out=a_bank[j][h][:],
                    lhsT=q_code[:, j * P : (j + 1) * P].bitcast(FP8X4),
                    lhsT_scale=q_scale[:, j * P : (j + 1) * P],
                    rhs=key_word[:, 2 * BANK * h : 2 * BANK * (h + 1)].bitcast(FP4X4),
                    rhs_scale=key_scale[:, BANK * h : BANK * (h + 1)],
                    start=True,
                    stop=True,
                )

        a_sb, c1, c2 = {}, {}, {}
        towards, negated = {}, {}

        def fetch_pair(step, j, window, towards_list, moved_list):
            pair = keep.tile([P, 2, I], F32, name="pair%d_%d" % (step, j))
            negated[step, j], towards[step, j] = pair[:, 0, :], pair[:, 1, :]
            nc.scalar.activation(negated[step, j], window[:].indirect(moved_list[:]), COPY, scale=-1.0)
            nc.scalar.activation(towards[step, j], window[:].indirect(towards_list[:]), COPY)

        def place(step, j, window, moved_list):
            nc.vector.tensor_tensor(window[:].indirect(moved_list[:]), towards[step, j], negated[step, j], ADD)

        def place_difference(step, j, window, moved_list, scaled):
            diff = keep.tile([P, I], F32, name="diff%d" % step)
            nc.gpsimd.tensor_tensor(diff[:], towards[step, j], negated[step, j], ADD)
            if scaled:
                moved_by = keep.tile([P, I], F32, name="moved_by%d_%d" % (step, j))
                nc.gpsimd.tensor_scalar(moved_by[:], diff[:], lam_sb[:, j : j + 1], 0.0, MULT, ADD)
                diff = moved_by
            nc.vector.tensor_copy(window[:].indirect(moved_list[:]), diff[:])

        def scores_out(j, shared):
            a_sb[j] = keep.tile([P, T], F32, name="wide%d" % j)
            if shared:
                nc.vector.tensor_copy(out=a_sb[j][:, :BANK], in_=a_bank[j][0][:])
            else:
                nc.scalar.copy(out=a_sb[j][:, :BANK], in_=a_bank[j][0][:])
            nc.scalar.copy(out=a_sb[j][:, BANK:], in_=a_bank[j][1][:])

        def settle1(j, placed, tag):
            c1[j] = keep.tile([P, T], F32, name=tag)
            for h in range(2):
                cols = slice(BANK * h, BANK * (h + 1))
                nc.vector.scalar_tensor_tensor(c1[j][:, cols], placed[:, cols], lam_sb[:, j : j + 1], a_bank[j][h][:], MULT, ADD)

        def settle2(j):
            c2[j] = keep.tile([P, T], F32, name=("pair2_3", "c1_0", "wide2", "c1_2")[j])
            if j == PACK - 1:
                nc.vector.scalar_tensor_tensor(c2[j][:], placed2[j % 3][:], lam_sb[:, j : j + 1], c1[j][:], MULT, ADD)
            else:
                nc.gpsimd.tensor_tensor(c2[j][:], placed2[j % 3][:], c1[j][:], ADD)

        scores_out(0, True)
        first_towards = [keep.tile([P, HALF], F32, name="first_towards%d" % h) for h in range(2)]
        first_negated = [keep.tile([P, HALF], F32, name="first_negated%d" % h) for h in range(2)]
        for h in range(2):
            cols = slice(HALF_COLS * h, HALF_COLS * (h + 1))
            nc.scalar.activation(first_negated[h][:], a_sb[0][:].indirect(list1[:, cols]), COPY, scale=-1.0)
            if h == 0:
                nc.vector.tensor_copy(first_towards[h][:], a_sb[0][:].indirect(list2[:, cols]))
            else:
                nc.scalar.activation(first_towards[h][:], a_sb[0][:].indirect(list2[:, cols]), COPY)
            if h == 1:
                scores_out(1, False)
            nc.vector.tensor_tensor(placed1[0][:].indirect(list1[:, cols]), first_towards[h][:], first_negated[h][:], ADD)
        settle1(0, placed1[0], "c1_0")

        fetch_pair(1, 1, a_sb[1], list2, list1)
        place(1, 1, placed1[1], list1)
        scores_out(2, False)
        fetch_pair(1, 2, a_sb[2], list2, list1)
        place(1, 2, placed1[0], list1)
        settle1(1, placed1[1], "wide2")
        settle1(2, placed1[0], "c1_2")
        scores_out(3, False)
        fetch_pair(1, 3, a_sb[3], list2, list1)
        place_difference(1, 3, placed1[1], list1, False)
        settle1(3, placed1[1], "c1_3")

        placed2 = [
            keep.tile([P, T], F32, name="q_bf", align_bytes=64),
            keep.tile([P, T], F32, name="wide0"),
            keep.tile([P, T], F32, name="wide1"),
        ]
        for tile in placed2:
            nc.gpsimd.memset(tile[:], 0.0)
        for j in range(PACK - 1):
            fetch_pair(2, j, c1[j], list3, list4)
            place_difference(2, j, placed2[j], list4, True)
        fetch_pair(2, PACK - 1, c1[PACK - 1], list3, list4)
        last_diff = keep.tile([P, I], F32, name="diff2")
        nc.gpsimd.tensor_tensor(last_diff[:], towards[2, PACK - 1], negated[2, PACK - 1], ADD)
        settle2(0)
        nc.vector.tensor_copy(placed2[0][:].indirect(list4[:]), last_diff[:])
        for j in range(1, PACK):
            settle2(j)

        last = PACK - 1
        rowf_wide = keep.tile([P, QUARTER], F32)
        nc.scalar.copy(out=rowf_wide[:], in_=rowf_sb[:, last : last + 1].to_broadcast([P, QUARTER]))
        gw_low = keep.tile([P, PACK, HALF], F32, name="gw_low", align_bytes=64)
        gw_bf = [keep.tile([P, HALF, PACK], BF16, name="gw_bf%d" % h, align_bytes=64) for h in range(2)]
        for j in range(last):
            g = keep.tile([P, I], F32, name="g%d" % j)
            nc.scalar.activation(g[:], c2[j][:].indirect(list2[:]), COPY)
            if j < last - 1:
                nc.scalar.activation(gw_low[:, j, :], g[:, :HALF], COPY, scale=rowf_sb[:, j : j + 1])
            else:
                nc.vector.tensor_scalar(gw_low[:, j, :], g[:, :HALF], rowf_sb[:, j : j + 1], None, MULT)
            nc.scalar.activation(gw_bf[1][:, :, j], g[:, HALF:], COPY, scale=rowf_sb[:, j : j + 1])
        for u in range(2):
            nc.vector.tensor_tensor(
                gw_low[:, last, QUARTER * u : QUARTER * (u + 1)],
                c2[last][:].indirect(list2[:, QUARTER_COLS * u : QUARTER_COLS * (u + 1)]),
                rowf_wide[:],
                MULT,
            )
        g_last = keep.tile([P, HALF], F32)
        nc.scalar.activation(g_last[:], c2[last][:].indirect(list2[:, HALF_COLS:]), COPY)
        nc.scalar.activation(gw_bf[1][:, :, last], g_last[:], COPY, scale=rowf_sb[:, last : last + 1])
        for u in range(2):
            slots = slice(QUARTER * u, QUARTER * (u + 1))
            nc.vector.tensor_copy(
                out=gw_bf[0][:, slots, :].rearrange("p (c i) t -> p c t i", i=4),
                in_=gw_low[:, :, slots].rearrange("p t (c i) -> p c t i", i=4),
            )
        for h in range(2):
            gw_code = keep.tile([P, HALF], U32, name="gw_low" if h else "gw_code0", align_bytes=64)
            gw_scale = keep.tile([P, HALF], U8, name="gw_scale%d" % h, align_bytes=64)
            width = HALF if h else QUARTER
            for lo in range(0, HALF, width):
                nc.vector.quantize_mx(
                    out=gw_code[:, lo : lo + width].bitcast(FP8X4),
                    scales=gw_scale[:, lo : lo + width],
                    in_=gw_bf[h][:, lo : lo + width, :].rearrange("p i t -> p (i t)"),
                )
            for e in range(E // P):
                y_bank = psum.tile([P, HALF], F32, name="bank%d" % (2 * h + e))
                nc.tensor.matmul_mx(
                    out=y_bank[:],
                    lhsT=mix_word[:, e * P : (e + 1) * P].bitcast(FP8X4),
                    lhsT_scale=mix_scale[:, e * P : (e + 1) * P],
                    rhs=gw_code[:].bitcast(FP8X4),
                    rhs_scale=gw_scale[:],
                    start=True,
                    stop=True,
                )
                y = keep.tile([P, HALF], F32, name="y%d_%d" % (h, e))
                if h == 1 and e == 1:
                    nc.vector.tensor_copy(out=y[:], in_=y_bank[:])
                else:
                    nc.scalar.copy(out=y[:], in_=y_bank[:])
                queue = nc.scalar if h == 1 and e == 0 else nc.sync
                queue.dma_start(out=out[e * P : (e + 1) * P, h * HALF : (h + 1) * HALF], in_=y[:])
